import numpy as np, ml_dtypes
CORES = [3,11,19,27,35,43]
N = 6
BF = ml_dtypes.bfloat16
W, S, PA, TH, E, R = 3584, 256, 1, 152, 14, 7
def near(rng, pro, kin, amp):
    v = pro[np.arange(8)[None, :, None], kin]; v = v + rng.integers(-amp, amp + 1, v.shape)
    return np.ascontiguousarray(np.minimum(np.maximum(v, 0), 255).transpose(0, 1, 3, 2))
def parts(rng, ends=False):
    pro = rng.integers(0, 256, (8, 3, 16))
    x = near(rng, pro, rng.integers(0, 3, (N, 8, S)), E); d = near(rng, pro, rng.integers(0, 3, (N, 8, W)), E)
    d = np.where(rng.random((N, 8, 1, W)) < 0.25, rng.integers(0, 256, d.shape), d)
    key = rng.random((N, 8, R, W))
    if ends: key[..., 0] = -1.0; key[..., W - 1] = -1.0
    a = np.argsort(key, axis=-1)[..., :S]
    a = rng.permuted(a, axis=-1)
    b = rng.integers(0, W, (N, 8, R, S)); o = rng.integers(0, W, (N, 8, 16, S)); k = rng.integers(0, 2 * R, o.shape)
    for r in range(N):
        for t in range(R): o[r] = np.where(k[r] == t, a[(r + t) % N, :, t][:, None, :], o[r])
    h = np.where(rng.random((N, 8, W)) < 0.5, grantors(rng, a, W), rng.integers(0, W, (N, 8, W)))
    return x, d, o, h, a, b
def grantors(rng, a, n):
    return np.take_along_axis(a.reshape(N, 8, R * S), rng.integers(0, R * S, (N, 8, n)), 2)
def pack(x, d, o, h, a, b):
    return {"own": np.ascontiguousarray(o).reshape(N, 128, S).astype(np.int32), "lm": np.ascontiguousarray(x).reshape(N, 128, S).astype(np.float32).astype(BF),
            "bk": np.ascontiguousarray(d).reshape(N, 128, W).astype(np.float32).astype(BF), "heir": np.ascontiguousarray(h).astype(np.int32),
            "da": np.ascontiguousarray(a).reshape(N, 8, R * S).astype(np.int32), "db": np.ascontiguousarray(b).reshape(N, 8, R * S).astype(np.int32)}
def setup_inputs(rng):
    return pack(*parts(rng))
def setup_inputs_ties(rng):
    x, d, o, h, a, b = parts(rng); mid = rng.integers(60, 196, (8, 16)); x = x * 0 + mid[None, :, :, None]
    s = TH + rng.integers(-1, 2, (N, 8, 1, W)); v = s // 16 + (np.arange(16)[None, None, :, None] < s % 16)
    u = rng.integers(0, (TH - 1) // 16 + 1, (N, 8, 8, W)); v[:, :, :8] += u; v[:, :, 8:] -= u
    d = mid[None, :, :, None] + v * (1 - 2 * rng.integers(0, 2, v.shape))
    return pack(x, d, o, h, a, b)
def setup_inputs_wake(rng):
    x, d, o, h, a, b = parts(rng); pro = rng.integers(40, 216, (8, 1, 16))
    x = near(rng, pro, np.zeros((N, 8, S), np.int64), E // 2); d = rng.integers(0, 256, d.shape)
    o1 = grantors(rng, a, 16 * S).reshape(o.shape); o2 = np.roll(grantors(rng, a, 16 * S), -1, axis=0).reshape(o.shape)
    o = np.where(rng.random(o.shape) < 0.6, o1, o2); h = grantors(rng, a, W); b = np.roll(grantors(rng, a, R * S), -1, axis=0).reshape(b.shape)
    return pack(x, d, o, h, a, b)
def setup_inputs_sleep(rng):
    x, d, o, h, a, b = parts(rng); m = rng.permutation(8); g = m[0]
    a[:, g] = 2 * np.argsort(rng.random((N, W // 2)), axis=-1)[:, :R * S].reshape(N, R, S); x[:, g, :, ::8] = 0
    o[:, g] = 2 * rng.integers(0, W // 2, (N, 16, S)) + 1; h[:, g] = 2 * rng.integers(0, W // 2, (N, W)) + 1; b[:, g] = 2 * rng.integers(0, W // 2, (N, R, S)) + 1
    g = m[1]; a[:, g] = np.argsort(rng.random((N, R, S)), axis=-1)
    o[:, g] = rng.integers(S, W, (N, 16, S)); h[:, g] = rng.integers(S, W, (N, W)); b[:, g] = rng.integers(S, W, (N, R, S))
    nxt = np.roll(a, -1, axis=0)
    for g in m[2:4]:
        x[:, g] = rng.integers(155, 256, (N, 16, S)); d[:, g] = rng.integers(0, 101, (N, 16, W)); b[:, g, :R - 1] = nxt[:, g, 1:]
    o[:, m[2]] = a[:, m[2], 0][:, None, :]; o[:, m[3], 15] = a[:, m[3], 0]
    pro = rng.integers(0, 256, (8, 1, 16)); xn = near(rng, pro, np.zeros((N, 8, S), np.int64), E // 4); dn = near(rng, pro, np.zeros((N, 8, W), np.int64), E // 4)
    for g in m[4:6]:
        x[:, g] = xn[:, g]; d[:, g] = dn[:, g]; h[:, g] = (np.arange(W) + 1) % W
    for r in range(N):
        o[r, m[4]] = rng.permutation((W - 1 - np.arange(16 * S)) % W).reshape(16, S)
        o[r, m[5]] = W - 1 - (r % 2) * rng.integers(0, W // 4, (16, S))
    return pack(x, d, o, h, a, b)
def setup_inputs_alike(rng):
    x, d, o, h, a, b = parts(rng, True); c = 255 * rng.integers(0, 2, (8, 16))[None, :, :, None]; q = rng.permutation(N)
    x = x * 0 + c; x[..., 1::2] = 255 - x[..., 1::2]; x[q[0]] = c[0]
    v = np.where(rng.random((N, 8, 1, W)) < 0.5, c, 255 - c); v[q[0]] = c[0]
    two = rng.random((N, 8, 1, W)) < 0.25; two[q[0]] = False
    s = np.where(two, rng.choice(np.array([128, 160]), two.shape), rng.choice(np.array([0, TH, TH, TH + 1, TH + 1, 255]), two.shape))
    s[q[0]] = rng.choice(np.array([0, TH, TH]), (8, 1, W))
    i = rng.integers(0, 16, two.shape); j = (i + rng.choice(np.array([1, 2, 4, 8, 8]), two.shape)) % 16; p = np.arange(16)[None, None, :, None]
    one = (p == i) | (two & (p == j)); d = v + np.where(v == 0, s, -s) * one
    few = np.array([0, W - 1, W // 2, 3]); o[:, ::2] = rng.choice(few, (N, 4, 16, S))
    h = np.where(rng.random(h.shape) < 0.4, rng.choice(few, h.shape), h); b = np.where(rng.random(b.shape) < 0.3, rng.choice(few, b.shape), b)
    b[..., ::16] = a[..., ::16]; o[q[1], :, 5] = a[q[1], :, 0]
    return pack(x, d, o, h, a, b)
def setup_inputs_spread(rng):
    x, d, o, h, a, b = parts(rng); pro = (np.exp2(8 * rng.random((8, 3, 16))) - 1).astype(np.int64)
    x = near(rng, pro, (3 * rng.random((N, 8, S)) ** 2).astype(np.int64), rng.integers(0, 2 * E + 1, (N, 8, S, 1)))
    d = near(rng, pro, (3 * rng.random((N, 8, W)) ** 2).astype(np.int64), rng.integers(0, 2 * E + 1, (N, 8, W, 1)))
    o = np.where(rng.random(o.shape) < 0.5, (W * rng.random(o.shape) ** 3).astype(np.int64), o)
    h = (W * rng.random(h.shape) ** 3).astype(np.int64); b = (W * rng.random(b.shape) ** 3).astype(np.int64)
    return pack(x, d, np.minimum(o, W - 1), np.minimum(h, W - 1), a, np.minimum(b, W - 1))
def check_inputs(d):
    bad = []
    for k in ("own", "heir", "da", "db"):
        if np.min(d[k]) < 0 or np.max(d[k]) > W - 1: bad.append("range of " + k)
    for k in ("lm", "bk"):
        v = np.asarray(d[k]).astype(np.float32)
        if not np.all((v >= 0) & (v <= 255) & (v == np.floor(v))): bad.append("whole numbers from 0 to 255 in " + k)
    s = np.sort(np.asarray(d["da"]).reshape(N, 8, R, S), axis=-1)
    if np.any(s[..., 1:] == s[..., :-1]): bad.append("different grantors in a round of a rank and group")
    return bad
def reference(own, lm, bk, heir, da, db):
    o = own.astype(np.int64).reshape(N, 8, 16, S); x = lm.astype(np.float32).astype(np.int32).reshape(N, 8, 16, S)
    d = bk.astype(np.float32).astype(np.int32).reshape(N, 8, 16, W); h = heir.astype(np.int64)
    for t in range(R):
        for r in range(N):
            c = (r + t) % N
            a = da[c][:, t * S:(t + 1) * S].astype(np.int64); b = db[c][:, t * S:(t + 1) * S].astype(np.int64)
            hit = o[r] == a[:, None, :]
            o[r] = np.where(hit, b[:, None, :], o[r])
            g, i = np.nonzero(~np.any(hit, axis=1))
            d[c][g, :, a[g, i]] = x[r][g, :, i]
            h[c][g, a[g, i]] = b[g, i]
            for s in range(PA):
                e = o[r].reshape(8, 16 * S)
                w = np.take_along_axis(d[c], e[:, None, :], 2).reshape(8, 16, 16, S)
                dist = np.add.reduce(np.abs(w - x[r][:, :, None, :]), axis=1)
                o[r] = np.where(dist <= TH, np.take_along_axis(h[c], e, 1).reshape(8, 16, S), o[r])
    return {"yo": o.reshape(N, 128, S).astype(np.float32), "yd": d.reshape(N, 128, W).astype(np.float32).astype(BF), "yh": h.astype(np.float32)}

from concourse.bass import DstId, RemoteDMATransfer
from concourse.mybir import AluOpType, AxisListType, ActivationFunctionType

N, W, S, R, TH = 6, 3584, 256, 7, 152
WX = W + 384
NMSG = 2 * (R - 1)
OFF = 4096.0
LIFT = 64.0
ROUND = 1.5 * 2 ** 23
HALF = 2048
A = AluOpType
F = ActivationFunctionType

SCRATCH = {
    "bk0": ("sbuf", [128, WX], "bfloat16"), "bk1": ("sbuf", [128, WX], "bfloat16"),
    "ax0": ("sbuf", [128, WX], "float32"), "ax1": ("sbuf", [128, WX], "float32"),
    "lx": ("sbuf", [128, 2 * N, 1024], "bfloat16"), "thr": ("sbuf", [128, N, 128], "float32"),
    "lmn": ("sbuf", [128, S], "bfloat16"),
    "land": ("sbuf", [128, NMSG, 128], "float32"), "snd": ("sbuf", [128, NMSG, 128], "float32"),
    "o0": ("sbuf", [128, 256], "float32"), "fin": ("sbuf", [128, 256], "float32"),
    "si": ("sbuf", [128, 2, 8, 16], "int32"), "sf": ("sbuf", [128, 2, 8, 16], "float32"),
    "s1": ("sbuf", [128, 2, 8, 16], "float32"),
    "ci": ("sbuf", [128, 448], "int32"),
    "chi": ("sbuf", [128, 448], "bfloat16"), "clo": ("sbuf", [128, 448], "bfloat16"),
    "npc": ("sbuf", [128, W + R * S], "bfloat16"),
    "athi": ("sbuf", [128, 512], "bfloat16"), "atlo": ("sbuf", [128, 512], "bfloat16"),
    "gm": ("sbuf", [128, 4, 1024], "bfloat16"), "ga": ("sbuf", [128, 4, 1024], "bfloat16"),
    "ou": ("sbuf", [128, 2, 128], "uint16"), "of": ("sbuf", [128, 2, 128], "float32"),
    "ofl": ("sbuf", [128, 2, 128], "float32"),
    "xo": ("sbuf", [128, 2, 16], "uint16"), "xt": ("sbuf", [128, 16], "float32"),
    "hit": ("sbuf", [128, 128], "bfloat16"), "cond": ("sbuf", [128, 128], "bfloat16"),
    "axc": ("sbuf", [128, 2, 256], "float32"),
    "yc": ("sbuf", [128, 2, 224], "float32"), "ys": ("sbuf", [128, 112], "float32"),
    "yf": ("sbuf", [128, 2, 112], "float32"),
    "oneb": ("sbuf", [128, 128], "bfloat16"), "monef": ("sbuf", [128, 128], "float32"),
    "mhalf": ("sbuf", [128, 8], "bfloat16"),
    "zz": ("sbuf", [128, 3, 144], "bfloat16"),
    "dup": ("sbuf", [128, 2, 128], "bfloat16"), "cs": ("sbuf", [128, 128], "bfloat16"),
    "lpair": ("sbuf", [128, 8, 16], "bfloat16"), "lh": ("sbuf", [128, 32, 16], "bfloat16"),
    "negi": ("sbuf", [128, 128], "float32"), "rr": ("sbuf", [128, 32], "bfloat16"),
    "sel": ("sbuf", [128, R, 128], "bfloat16"), "dm": ("sbuf", [128, 16], "float32"),
    "gb": ("sbuf", [128, 2], "float32"),
}
for _i in range(8):
    SCRATCH["p%d" % _i] = ("psum", [128, 512], "float32")

SEMAPHORES = (["cv", "ca", "cp", "cg", "sent", "ldo", "ldc", "ldl", "ldb0a", "ldb0b", "ldb1a", "dnp", "yc0", "yc1", "st"]
              + ["arr%d" % i for i in range(NMSG)] + ["lf%d" % i for i in range(1, N)]
              + ["r1_%d" % i for i in range(1, N)] + ["r2_%d" % i for i in range(1, N)])


def rank_program(g, core, T, topo):
    rank = T.rank_of(core)
    if rank is None:
        return
    eng = {"v": g.vector, "a": g.scalar, "p": g.tensor, "g": g, "s": g.sync}
    csem = {"v": "cv", "a": "ca", "p": "cp", "g": "cg"}
    ops, lastw, readers, touch, total = [], {}, {}, {}, {}

    def op(q, fn, r=(), w=(), bank=None, sem=None, n=0):
        deps = set()
        for k in r:
            if k in lastw:
                deps.add(lastw[k])
        for k in w:
            if k in lastw:
                deps.add(lastw[k])
            deps.update(readers.get(k, ()))
        if bank is not None:
            for q2, i2 in touch.get(bank, {}).items():
                if q2 != q:
                    deps.add(i2)
        me = len(ops)
        latest = {}
        for d in deps:
            o = ops[d]
            if (q == "p" and o["q"] == "p") or (sem is not None and o["sem"] == sem):
                continue
            key = o["sem"] or csem[o["q"]]
            latest[key] = max(latest.get(key, 0), d)
        if sem is not None:
            total[sem] = total.get(sem, 0) + n
        ops.append({"q": q, "fn": fn, "deps": sorted(latest.values()), "sem": sem, "need": False})
        for k in r:
            readers.setdefault(k, []).append(me)
        for k in w:
            lastw[k] = me
            readers[k] = []
        if bank is not None:
            touch.setdefault(bank, {})[q] = me

    def dma(q, out, in_, sem, r=(), w=()):
        op(q, lambda e: e.dma_start(out, in_).then_inc(T.sem[sem], 16), r, w, sem=sem, n=16)

    def mm(b, out, lhsT, rhs, start, stop, r):
        op("p", lambda e: e.matmul(out, lhsT, rhs, start, stop), r, ["p%d" % b], bank=b)

    def asel(out, in_, pattern, cmp, fill, base, r, w):
        op("g", lambda e: e.affine_select(out, in_, pattern, cmp, fill, base, 1), r, w)

    def nsel(out, in_, pattern, cmp, fill, base, r, w):
        op("g", lambda e: e.affine_select(out, in_, pattern, cmp, fill, base, -1), r, w)

    P = [T["p%d" % i] for i in range(8)]
    BK, AX = [T.bk0, T.bk1], [T.ax0, T.ax1]
    BKEY = [["bk0a", "bk0b"], ["bk1a"]]

    dma("s", T.ci[:, 0:224], T.heir[:], "ldc", w=["ci"])
    dma("a", T.ci[0:64, 224:448], T.db[:], "ldc", w=["ci1"])
    dma("a", T.ci[64:128, 224:448], T.da[:], "ldc", w=["ci2"])
    dma("s", T.lmn[:], T.lm[:], "ldl", w=["lmn"])
    for b in range(2):
        for x in range(2):
            dma("sa"[x], T.si[x::2, b], T.own[b::2, 128 * x:128 * x + 128], "ldo", w=["si%d%d" % (b, x)])

    def load_book(y, qs, c0, c1, key):
        for G in range(4):
            for b in range(2):
                dma(qs[b], BK[y][32 * G + 16 * b:32 * G + 16 * b + 16, c0:c1], T.bk[32 * G + 16 * y:32 * G + 16 * y + 16, c0:c1],
                    "ld" + key[0] + key[2:], w=[key])
    load_book(0, "sa", 0, HALF, "bk0a")

    def mset(ap, val, k):
        op("v", lambda e: e.memset(ap, val), w=k)
    mset(T.oneb[:], 1.0, ["oneb"])
    mset(T.zz[:], 0.0, ["z1", "zd", "zh"])
    mset(T.lpair[:], 0.0, ["lpair"])
    mset(T.lh[0:32], 0.0, ["lh0", "lh1", "lh2", "lh3"])
    mset(T.rr[0:32], 0.0, ["rr0", "rr1"])
    mset(T.mhalf[:], -0.5, ["mhalf"])
    mset(T.monef[:], -1.0, ["monef"])
    z1, zd, zh = T.zz[:, 0, 15:143:16], T.zz[:, 1, 15:143:16], T.zz[:, 2, 15:143:16]
    gpat = [[-1, 2], [-2, 4], [0, 2]]

    def make_rr(kind, row, val):
        ap = T.rr[0:32, 16 * kind:16 * kind + 16]
        asel(ap, ap, gpat, A.not_equal, val, -row, ["rr%d" % kind], ["rr%d" % kind])

    def make_lh(k):
        asel(T.lh[0:32, 8 * k:8 * k + 8, 8:10], T.oneb[0:32, 0:16], [[-2, 4], [0, 2], [-8 * (1 + k // 2), 2]], A.is_equal, 0.0,
             -(k % 2), ["oneb"], ["lh%d" % k])

    def make_sel(t):
        asel(T.sel[:, t], T.oneb[:], [[0, 8], [-1, 16]], A.is_equal, 0.0, -16 * t, ["oneb"], ["sel%d" % t])
    for y in range(2):
        asel(T.dup[:, y], T.oneb[:], [[-32, 4], [0, 2], [-1, 16]], A.is_equal, 0.0, -16 * y, ["oneb"], ["dup%d" % y])
    asel(z1, T.oneb[:, 0:8], [[-16, 8]], A.is_ge, 0.0, 0, ["oneb"], ["z1"])
    asel(T.lpair[:, :, 0:8], T.oneb[:, 0:64], [[-16, 8], [-2, 8]], A.is_ge, 0.0, 0, ["oneb"], ["lpair"])
    nsel(z1, z1, [[16, 8]], A.is_ge, 0.0, 15, ["z1"], ["z1"])
    nsel(T.lpair[:, :, 0:8], T.lpair[:, :, 0:8], [[16, 8], [2, 8]], A.is_ge, 0.0, 1, ["lpair"], ["lpair"])
    make_rr(1, 0, 1.0)
    make_rr(0, 8, 1.0)
    make_rr(1, 16, 1.0)
    make_rr(0, 24, 1.0)
    make_rr(1, 8, -1.0)
    make_lh(0)
    make_rr(1, 24, -1.0)
    make_sel(0)
    make_lh(2)
    op("g", lambda e: e.iota(T.dm[:], [[16, 16]], W + int(OFF), 1, allow_small_or_imprecise_dtypes=True), w=["dm"])
    asel(zd, T.mhalf[:], [[-16, 8]], A.is_ge, 0.0, 0, ["mhalf"], ["zd"])
    asel(zh, T.oneb[:, 0:8], [[-16, 8]], A.is_ge, 0.0, -8, ["oneb"], ["zh"])
    nsel(zd, zd, [[16, 8]], A.is_ge, 0.0, 7, ["zd"], ["zd"])
    nsel(zh, zh, [[16, 8]], A.is_ge, 0.0, 9, ["zh"], ["zh"])
    make_lh(1)
    asel(zh, zh, [[-16, 8]], A.not_equal, -2.0, -10, ["zh"], ["zh"])
    make_lh(3)
    asel(T.negi[:], T.monef[:], [[-1, 128]], A.is_equal, 0.0, 0, ["monef"], ["negi"])

    op("v", lambda e: e.tensor_scalar(P[4][:, 0:448], T.ci[:], OFF, None, A.add), ["ci", "ci1", "ci2"], ["p4"], bank=4)
    op("a", lambda e: e.activation(T.chi[:], P[4][:, 0:448], F.Copy), ["p4"], ["chi"], bank=4)
    op("v", lambda e: e.tensor_scalar(T.sf[:], T.si[:], OFF, None, A.add), ["si00", "si01", "si10", "si11"], ["sf"])
    op("v", lambda e: e.tensor_tensor(T.clo[:], P[4][:, 0:448], T.chi[:], A.subtract), ["p4", "chi"], ["clo"], bank=4)
    dma("s", T.npc[0:16, W:W + R * S], T.chi[:, 224:448], "dnp", ["chi"], ["np0"])
    dma("s", T.npc[0:8, 0:W], T.chi[:, 0:224], "dnp", ["chi"], ["np1"])
    dma("s", T.npc[16:32, W:W + R * S], T.clo[:, 224:448], "dnp", ["clo"], ["np2"])
    dma("s", T.npc[8:16, 0:W], T.clo[:, 0:224], "dnp", ["clo"], ["np3"])
    NP = ["np0", "np1", "np2", "np3"]
    load_book(0, "ss", HALF, W, "bk0b")
    load_book(1, "ss", 0, W, "bk1a")

    for y in range(2):
        mm(6, P[6][:, 256 * y:256 * y + 256], T.dup[:, y], T.lmn[:], True, True, ["dup%d" % y, "lmn"])
    for y in range(2):
        for k in range(4):
            op("a", lambda e, y=y, k=k: e.activation(T.lx[:, y, 256 * k:256 * k + 256], P[6][:, 256 * y:256 * y + 256], F.Copy),
               ["p6"], ["lx%d_%d" % (y, k)], bank=6)
        for p in range(16):
            mm(5, P[5][:, 64 * y:64 * y + 64], T.zz[:, 0, 15 - p:143 - p], T.lx[:, y, p::16], p == 0, p == 15,
               ["z1"] + ["lx%d_%d" % (y, k) for k in range(4)])
    for c in range(8):
        op("v", lambda e, c=c: e.transpose(T.o0[:, c::8], T.sf[:, :, c, :]), ["sf"], ["o0_%d" % c])
    O0 = ["o0_%d" % c for c in range(8)]
    op("v", lambda e: e.tensor_tensor(T.cs[:], T.dup[:, 0], T.dup[:, 1], A.add), ["dup0", "dup1"], ["cs"])
    op("v", lambda e: e.tensor_scalar(T.cs[:], T.cs[:], OFF, None, A.mult), ["cs"], ["cs"])
    op("v", lambda e: e.tensor_scalar(T.thr[:, 0], P[5][:, 0:128], 0.5, (8 * 255 + TH + 0.5) / 2, A.mult, A.add), ["p5"], ["thr0"], bank=5)

    for p in range(16):
        mm(7, P[7][0:112, p::16], T.npc[0:32, W + p::16], T.rr[0:32, :], True, True, ["np0", "np2", "rr0", "rr1"])

    def lxk(s):
        j = 2 * ((s // 2) % N) + s % 2
        return j, ["lx%d_0" % j], ["lx%d_%d" % (j, k) for k in range(4)]

    def prep_deed(s):
        t, y = s // 2, s % 2
        at = ["athi", "atlo", "sel%d" % t]
        for kind in range(2):
            c0 = 256 * kind + 128 * y
            mm(2, P[2][:, 128 * kind:128 * kind + 128], T.athi[0:112, c0:c0 + 128], T.sel[0:112, t], True, False, at)
            mm(2, P[2][:, 128 * kind:128 * kind + 128], T.atlo[0:112, c0:c0 + 128], T.sel[0:112, t], False, True, at)
        mm(3, P[3][:, 0:16], T.athi[0:112, 128 * y:128 * y + 128], T.sel[0:112, t, 0:16], True, False, at)
        mm(3, P[3][:, 0:16], T.atlo[0:112, 128 * y:128 * y + 128], T.sel[0:112, t, 0:16], False, False, at)

    def prep_ax(s):
        t, y = s // 2, s % 2
        j, k0, k1 = lxk(s)
        mm(4, P[4][:, 0:256], T.lpair[:], T.lx[:, j, 0:256], True, False, ["lpair"] + k0)
        mm(4, P[4][:, 0:256], T.lh[0:32, 16 + 8 * y:24 + 8 * y], T.npc[0:32, W + S * t:W + S * t + S], False, True,
           ["lh%d" % (2 + y)] + NP)

    def copy_ax(s):
        y = s % 2
        op("a", lambda e: e.activation(T.axc[:, y], P[4][:, 0:256], F.Identity, bias=LIFT), ["p4"], ["axc%d" % y], bank=4)

    prv, nxt = T.cores[(rank - 1) % N], T.cores[(rank + 1) % N]

    def deed(s):
        t, y = s // 2, s % 2
        if t == 0:
            new, kn = T.o0[:, 128 * y:128 * y + 128], O0
        else:
            new, kn = T.land[:, s - 2], ["land%d" % (s - 2)]
            op(None, None, w=kn, sem="arr%d" % (s - 2), n=2 * len(topo.engines(prv, core)))

        def hit():
            op("v", lambda e: e.tensor_tensor(T.hit[:], new, P[2][:, 0:128], A.is_equal), kn + ["p2"], ["hit"], bank=2)
            for q in range(8):
                mm(3, P[3][:, 0:16], T.cs[:], T.hit[:, 16 * q:16 * q + 16], False, q == 7, ["cs", "hit"])
        return {
            "hit": hit,
            "t2": lambda: op("v", lambda e: e.tensor_tensor(P[2][:, 256:384], T.hit[:], P[2][:, 128:256], A.mult),
                             ["hit", "p2"], ["t2"], bank=2),
            "of": lambda: op("v", lambda e: e.tensor_tensor(T.of[:, y], new, P[2][:, 256:384], A.add),
                             kn + ["t2"], ["of%d" % y], bank=2),
            "ou": lambda: op("v", lambda e: e.tensor_scalar(T.ou[:, y], T.of[:, y], -OFF, None, A.add), ["of%d" % y], ["ou%d" % y]),
            "xt": lambda: op("v", lambda e: e.tensor_tensor(T.xt[:], T.dm[:], P[3][:, 0:16], A.min), ["p3", "dm"], ["xt"], bank=3),
            "xo": lambda: op("v", lambda e: e.tensor_scalar(T.xo[:, y], T.xt[:], -OFF, None, A.add), ["xt"], ["xo%d" % y]),
        }

    def scatter(s):
        y = s % 2
        j, k0, k1 = lxk(s)
        op("v", lambda e: e.tensor_copy(BK[y][:, 0:WX].indirect(T.xo[:, y]), T.lx[:, j, 0:256]), ["xo%d" % y] + k0, BKEY[y])
        op("a", lambda e: e.activation(AX[y][:, 0:WX].indirect(T.xo[:, y]), T.axc[:, y], F.Silu),
           ["xo%d" % y, "axc%d" % y] + ["axi%d_%d" % (y, i) for i in range(7)], ["ax%d" % y])

    def gather(s, c):
        y = s % 2
        j, k0, k1 = lxk(s)
        off = T.ou[:, y, 64 * c:64 * c + 64]
        op("v", lambda e: e.tensor_tensor(T.gm[:, 2 * y + c], BK[y][:, 0:W].indirect(off), T.lx[:, j], A.max),
           BKEY[y] + ["ou%d" % y] + k1, ["gm%d" % (2 * y + c)])
        op("a", lambda e: e.activation(T.ga[:, 2 * y + c], AX[y][:, 0:W].indirect(off), F.Identity, bias=T.gb[:, 1:2]),
           ["ax%d" % y, "ou%d" % y, "gb"], ["ga%d" % (2 * y + c)])

    def pe_heir(s, c):
        y = s % 2
        mm(c, P[c][:, 64:128], T.negi[:], T.of[:, y, 64 * c:64 * c + 64], True, False, ["negi", "of%d" % y])
        for p in range(16):
            mm(c, P[c][:, 64:128], T.zz[:, 2, 15 - p:143 - p], T.ga[:, 2 * y + c, p::16], False, p == 15, ["zh", "ga%d" % (2 * y + c)])

    def pe_dist(s, c):
        y = s % 2
        for p in range(16):
            mm(c, P[c][:, 0:64], T.zz[:, 1, 15 - p:143 - p], T.ga[:, 2 * y + c, p::16], p == 0, False, ["zd", "ga%d" % (2 * y + c)])
        for p in range(16):
            mm(c, P[c][:, 0:64], T.zz[:, 0, 15 - p:143 - p], T.gm[:, 2 * y + c, p::16], False, p == 15, ["z1", "gm%d" % (2 * y + c)])

    def decode(s, c):
        y, j = s % 2, (s // 2) % N
        last = s >= NMSG
        cols = slice(64 * c, 64 * c + 64)
        if last:
            out, old, ko = T.fin[:, 128 * y + 64 * c:128 * y + 64 * c + 64], T.ofl[:, y, cols], "ofl%d" % y
        else:
            out, old, ko = T.snd[:, s, cols], T.of[:, y, cols], "of%d" % y

        def new():
            op("v", lambda e: e.tensor_tensor(out, old, P[c][:, 128:192], A.add), ["t%d" % c, ko], ["snd%d_%d" % (s, c)], bank=c)
            if not last:
                rid, pid = topo.addr(nxt)[0:2]
                op("g", lambda e: e.remote_dma(T.land[:, s, cols], out, T.sem["arr%d" % s], T.sem.sent, pid, rid, topo.mask(core, nxt)),
                   ["snd%d_%d" % (s, c)], sem="sent", n=len(topo.engines(core, nxt)))
        return {
            "cond": lambda: op("v", lambda e: e.tensor_tensor(T.cond[:, cols], P[c][:, 0:64], T.thr[:, j, 64 * y:64 * y + 64], A.is_le),
                               ["p%d" % c, "thr%d" % j], ["cond%d" % c], bank=c),
            "t": lambda: op("v", lambda e: e.tensor_tensor(P[c][:, 128:192], T.cond[:, cols], P[c][:, 64:128], A.mult),
                            ["p%d" % c, "cond%d" % c], ["t%d" % c], bank=c),
            "new": new,
        }

    def send_lm(t):
        dst = T.cores[(rank + t) % N]
        rid, pid = topo.addr(dst)[0:2]
        en = topo.engines(core, dst)
        h = len(en) // 2
        trs = [RemoteDMATransfer(dst_ids=[DstId(rid=rid, pnc=pid)], dma_engine_mask=sum(1 << e for e in en[h * y:h * y + h]),
                                 remote_sem=T.sem["lf%d" % t], src=T.lx[:, y, 0:256], dst=T.lx[:, 2 * t + y, 0:256])
               for y in range(2)]
        op("g", lambda e: e.remote_dma_fused(trs, local_sem=T.sem.sent), ["lx0_0", "lx1_0"], sem="sent", n=2 * h)
        op("g", lambda e: e.remote_dma(T.thr[:, t], T.thr[:, 0], T.sem["lf%d" % t], T.sem.sent, pid, rid, topo.mask(core, dst)),
           ["thr0"], sem="sent", n=len(en))

    def recv_lm(t):
        ne = len(topo.engines(T.cores[(rank - t) % N], core))
        k = [["lx%d_%d" % (2 * t + y, i) for y in range(2)] for i in range(4)]
        op(None, None, w=k[0] + ["thr%d" % t], sem="lf%d" % t, n=2 * (ne // 2) + ne)
        dma("s", T.lx[:, 2 * t:2 * t + 2, 256:512], T.lx[:, 2 * t:2 * t + 2, 0:256], "r1_%d" % t, k[0], k[1])
        dma("s", T.lx[:, 2 * t:2 * t + 2, 512:1024], T.lx[:, 2 * t:2 * t + 2, 0:512], "r2_%d" % t, k[0] + k[1], k[2] + k[3])

    def init_mm(y, i, b):
        key = BKEY[y][-1] if 512 * i >= HALF else BKEY[y][0]
        mm(b, P[b][:], T.lpair[:], BK[y][:, 512 * i:512 * i + 512], True, False, ["lpair", key])
        mm(b, P[b][:], T.lh[0:16, 8 * y:8 * y + 8], T.npc[0:16, 512 * i:512 * i + 512], False, True, ["lh%d" % y] + NP)

    def init_copy(y, i, b, q):
        out = AX[y][:, 512 * i:512 * i + 512]
        if q == "a":
            op("a", lambda e: e.activation(out, P[b][:], F.Identity, bias=LIFT), ["p%d" % b], ["axi%d_%d" % (y, i)], bank=b)
        else:
            op("v", lambda e: e.tensor_scalar(out, P[b][:], LIFT, None, A.add), ["p%d" % b], ["axi%d_%d" % (y, i)], bank=b)

    def init(y, i, b, q):
        init_mm(y, i, b)
        init_copy(y, i, b, q)

    def out_books(y):
        dma("s", T.yc[:, y, 0:112], AX[y][8::32, 0:W], "yc%d" % y, ["ax%d" % y], ["ych%d" % y])
        dma("s", T.yc[:, y, 112:224], AX[y][9::32, 0:W], "yc%d" % y, ["ax%d" % y], ["ycl%d" % y])
        for G in range(4):
            dma("s", T.yd[32 * G + 16 * y:32 * G + 16 * y + 16, :], BK[y][32 * G:32 * G + 16, 0:W], "st", BKEY[y])

    def sum_heirs(y):
        for k in range(2):
            mm(5, P[5][:, 0:112], T.negi[:], T.yc[:, y, 112 * k:112 * k + 112], k == 0, k == 1, ["negi", "ych%d" % y, "ycl%d" % y])

    def out_heirs(y):
        op("a", lambda e: e.activation(T.ys[:], P[5][:, 0:112], F.Identity, bias=ROUND, scale=-1.0), ["p5"], ["ys"], bank=5)
        op("a", lambda e: e.activation(T.yf[:, y], T.ys[:], F.Identity, bias=-(ROUND + OFF + 2 * LIFT)), ["ys"], ["yf%d" % y])
        dma("s", T.yh[y::2, :], T.yf[:, y], "st", ["yf%d" % y])

    send_lm(1)
    make_sel(1)
    op("v", lambda e: e.tensor_reduce(T.gb[:, 0:1], zd, AxisListType.X, A.add), ["zd"], ["gb0"])
    op("a", lambda e: e.activation(T.athi[0:112, :], P[7][0:112, :], F.Copy), ["p7"], ["athi"], bank=7)
    op("v", lambda e: e.tensor_scalar(T.gb[:, 1:2], T.gb[:, 0:1], 2 * (255 + LIFT), None, A.mult), ["gb0"], ["gb"])
    op("v", lambda e: e.tensor_tensor(T.atlo[0:112, :], P[7][0:112, :], T.athi[0:112, :], A.subtract), ["p7", "athi"], ["atlo"], bank=7)
    prep_ax(0)
    init(0, 0, 0, "a")
    init(0, 1, 1, "a")
    prep_deed(0)
    init_mm(0, 2, 6)
    dd = deed(0)
    for k in ("hit", "t2", "of", "xt", "ou", "xo"):
        dd[k]()
    init_copy(0, 2, 6, "a")
    copy_ax(0)
    init(0, 3, 5, "v")
    init(0, 4, 0, "a")
    init(0, 5, 1, "v")
    init(0, 6, 7, "a")
    recv_lm(1)
    for s in range(2 * R):
        t, y = s // 2, s % 2
        more = s + 1 < 2 * R
        scatter(s)
        if s > 0:
            d1 = decode(s - 1, 1)
            for k in ("cond", "t", "new"):
                d1[k]()
        if y == 1 and t + 2 < N:
            send_lm(t + 2)
            recv_lm(t + 2)
        if y == 1 and t + 2 < R:
            make_sel(t + 2)
        if t == R - 1:
            out_books(y)
        if more:
            prep_deed(s + 1)
            prep_ax(s + 1)
        else:
            sum_heirs(0)
        if s == 0:
            for i, b in enumerate((5, 6, 7, 1)):
                init_mm(1, i, b)
        gather(s, 0)
        if s == 0:
            init_copy(1, 0, 5, "v")
            init_copy(1, 1, 6, "v")
        pe_heir(s, 0)
        if s == 0:
            init_mm(1, 4, 5)
        pe_dist(s, 0)
        if s == 0:
            init_mm(1, 5, 6)
        gather(s, 1)
        if s == 0:
            init_copy(1, 3, 1, "a")
            init_copy(1, 2, 7, "a")
        if more:
            copy_ax(s + 1)
        else:
            out_heirs(0)
        if t == R - 1:
            op("a", lambda e, y=y: e.activation(T.ofl[:, y], T.of[:, y], F.Identity, bias=-OFF), ["of%d" % y], ["ofl%d" % y])
        if s > 0:
            pe_heir(s, 1)
        d0 = decode(s, 0)
        if more:
            dd = deed(s + 1)
            for f in (d0["cond"], dd["hit"], d0["t"], dd["t2"], d0["new"], dd["of"], dd["xt"], dd["ou"], dd["xo"]):
                f()
        else:
            for k in ("cond", "t", "new"):
                d0[k]()
        if s == 0:
            init_mm(1, 6, 7)
            init_copy(1, 4, 5, "a")
            init_copy(1, 5, 6, "a")
            init_copy(1, 6, 7, "a")
            pe_heir(s, 1)
        pe_dist(s, 1)
    sum_heirs(1)
    d1 = decode(2 * R - 1, 1)
    for k in ("cond", "t", "new"):
        d1[k]()
    out_heirs(1)
    FIN = ["snd%d_%d" % (s, c) for s in (2 * R - 2, 2 * R - 1) for c in range(2)]
    for c in range(8):
        op("v", lambda e, c=c: e.transpose(T.s1[:, :, c, :], T.fin[:, c::8]), FIN, ["s1_%d" % c])
    for b in range(2):
        for x in range(2):
            dma("sa"[x], T.yo[b::2, 128 * x:128 * x + 128], T.s1[x::2, b], "st", ["s1_%d" % c for c in range(8)])

    for o in ops:
        for d in o["deps"]:
            ops[d]["need"] = True
    count, mark = {}, {}
    for i, o in enumerate(ops):
        if o["sem"] is None and o["need"]:
            count[o["q"]] = count.get(o["q"], 0) + 1
            mark[i] = count[o["q"]]
    waited, seen = {}, {}
    for i, o in enumerate(ops):
        q = o["q"]
        if q is None:
            continue
        for d in o["deps"]:
            sn = ops[d]["sem"] or csem[ops[d]["q"]]
            val = total[sn] if ops[d]["sem"] else mark[d]
            if waited.get((q, sn), 0) < val:
                eng[q].wait_ge(T.sem[sn], val)
                waited[(q, sn)] = val
                seen[sn] = max(seen.get(sn, 0), val)
        ins = o["fn"](eng[q])
        if i in mark:
            ins.then_inc(T.sem[csem[q]], 1)
    for q in count:
        total[csem[q]] = count[q]
    for sn in sorted(total):
        if seen.get(sn, 0) < total[sn]:
            g.sync.wait_ge(T.sem[sn], total[sn])
